import numpy as np
import ml_dtypes


def mxq(x, axis, fmt="e4m3"):
    dtype, down = {"e4m3": (ml_dtypes.float8_e4m3fn, 7), "e5m2": (ml_dtypes.float8_e5m2, 14)}[fmt]
    v = np.moveaxis(np.asarray(x, np.float32).astype(ml_dtypes.bfloat16).astype(np.float64), axis, -1)
    blocks = v.reshape(v.shape[:-1] + (-1, 32))
    amax = np.abs(blocks).max(-1, keepdims=True)
    byte = np.maximum(np.where(amax > 0, np.frexp(amax)[1] - 1 + 127, 0) - down, 1)
    scale = np.exp2(byte - 127.0)
    codes = (blocks / scale).astype(np.float32).astype(dtype).astype(np.float64)
    return np.moveaxis((codes * scale).reshape(v.shape), -1, axis)


WIDE = False


def mx_kscale(k):
    if not WIDE:
        return np.ones(k)
    levels = np.array([10, -10, 5, -5, 0])
    if k % 512:
        return np.exp2(np.random.permutation(np.resize(levels, k // 32))).repeat(32)
    a = np.empty((k // 512, 16))
    for p in range(k // 512):
        a[p, :8] = np.random.permutation(np.resize(levels, 8))
        for g in range(8):
            far = levels[np.abs(levels - a[p, g]) >= 10]
            a[p, g + 8] = far[np.random.randint(len(far))]
    return np.exp2(a.ravel()).repeat(32)


def f64(x):
    return np.asarray(x).astype(np.float64)


def striped(idx):
    return np.tile(idx.reshape(-1, 16).T, (8, 1)).astype(np.uint16)


def unstriped(offs):
    return offs[:16].T.reshape(-1).astype(np.int64)


def striped8(idx):
    return np.concatenate([x.reshape(-1, 16).T for x in idx]).astype(np.uint16)


def runs(offs, k):
    lists = np.stack([offs[16 * r : 16 * r + 16].T.reshape(-1) for r in range(8)]).astype(np.int64)
    return lists[np.arange(k) % 512 // 64]


def pack_weight(w):
    k, n = w.shape
    w = f64(np.asarray(w, np.float32).astype(ml_dtypes.bfloat16)).reshape(k // 32, 32, n)
    amax = np.abs(w).max(1)
    byte = np.clip(np.where(amax > 0, np.frexp(amax)[1] - 1 + 127 - 7, 1), 1, 254)
    scaled = (w * np.exp2(127.0 - byte)[:, None, :]).reshape(k, n).astype(np.float32)
    words = np.ascontiguousarray(scaled.reshape(k // 512, 128, 4, n).transpose(0, 1, 3, 2)).astype(ml_dtypes.float8_e4m3fn).view(np.uint8)
    return words, np.ascontiguousarray(byte.astype(np.uint8).reshape(k // 512, 16, n))


def unpack_weight(words, scales):
    g, p, n, _ = words.shape
    vals = np.ascontiguousarray(words).view(ml_dtypes.float8_e4m3fn).astype(np.float64) * np.repeat(np.exp2(scales.astype(np.float64) - 127.0), 8, axis=1)[..., None]
    return vals.transpose(0, 1, 3, 2).reshape(g * 512, n)


K, T, S, N, G, H, J = 512, 1024, 512, 512, 2048, 512, 512


def setup_inputs():
    n = np.random.standard_normal
    s = mx_kscale(K)[:, None]
    u = mx_kscale(S)
    packed_xT = pack_weight(n((K, T)) * s)
    packed_dT = pack_weight(n((K, G)) / s)
    return {
        "x_words": packed_xT[0],
        "x_scales": packed_xT[1],
        "d_words": packed_dT[0],
        "d_scales": packed_dT[1],
        "tab": n((H, J)).astype(np.float32),
        "gn": (np.random.uniform(0.5, 1.5, (H, 1)) * u[:, None]).astype(np.float32),
        "gm": (np.random.uniform(0.5, 1.5, (H, 1)) * u[:, None]).astype(np.float32),
        "w1": (n((H, N)) / np.sqrt(2 * H) / u[:, None]).astype(np.float32),
        "w2": (n((H, N)) / np.sqrt(2 * H) / u[:, None]).astype(np.float32),
        "tab2": np.random.uniform(0.4, 1.4, (N, J)).astype(np.float32),
        "offs": striped(np.random.permutation(T)[:S]),
        "k1": striped8(np.random.randint(0, G, (8, H))),
        "two": striped(np.random.permutation(T)[:S]),
        "k2": striped8(np.random.randint(0, G, (8, H))),
        "n1": striped8(np.stack([np.random.permutation(S) for _ in range(8)])),
        "n2": striped8(np.stack([np.random.permutation(S) for _ in range(8)])),
        "n3": striped8(np.random.randint(0, J, (8, S))),
        "n4": striped8(np.random.randint(0, J, (8, S))),
        "n5": striped8(np.stack([np.random.permutation(S) for _ in range(8)])),
        "n6": striped8(np.random.randint(0, J, (8, S))),
        "n7": striped8(np.stack([np.random.permutation(S) for _ in range(8)])),
    }


def reference(x_words, x_scales, d_words, d_scales, tab, gn, gm, w1, w2, tab2, offs, k1, two, k2, n1, n2, n3, n4, n5, n6, n7):
    d_k1 = unpack_weight(d_words, d_scales)[np.arange(K)[:, None], runs(k1, K)]
    xq = unpack_weight(x_words, x_scales)[:, unstriped(offs)]
    a = 0.0625 * (d_k1.T @ xq)
    st = a + a[np.arange(H)[:, None], runs(n1, H)]
    z = f64(gn) * (st * (np.tanh(st[np.arange(H)[:, None], runs(n2, H)])))
    d_k2 = unpack_weight(d_words, d_scales)[np.arange(K)[:, None], runs(k2, K)]
    x_two = unpack_weight(x_words, x_scales)[:, unstriped(two)]
    b = 0.0625 * (d_k2.T @ x_two)
    z2 = f64(gm) * ((b[np.arange(H)[:, None], runs(n5, H)]) * (f64(tab)[np.arange(H)[:, None], runs(n3, H)]) + f64(tab)[np.arange(H)[:, None], runs(n4, H)])
    h = mxq(f64(w1), 0, "e4m3").T @ mxq(z, 0, "e4m3") + mxq(f64(w2), 0, "e4m3").T @ mxq(z2, 0, "e4m3")
    return h * (f64(tab2)[np.arange(N)[:, None], runs(n6, N)]) - (0.5 * (h[np.arange(N)[:, None], runs(n7, N)]))

@@ -1,0 +1,308 @@
+from contextlib import ExitStack
+
+import concourse.mybir as mybir
+
+F32 = mybir.dt.float32
+BF16 = mybir.dt.bfloat16
+I32 = mybir.dt.int32
+U32 = mybir.dt.uint32
+U16 = mybir.dt.uint16
+U8 = mybir.dt.uint8
+FP8X4 = mybir.dt.float8_e4m3fn_x4
+ALU = mybir.AluOpType
+ACT = mybir.ActivationFunctionType
+
+P = 128
+PACK = 4
+S = 512
+T = 1024
+G = 2048
+WIN = 1024
+SHIFT = 14
+FLOPS = 4 * 2 * 512 * 512 * 512
+
+
+def tile_picked_pqjhoppkindakindg_none_p_kernel(
+    tc, x_words, x_scales, d_words, d_scales, tab, gn, gm, w1, w2, tab2,
+    offs, k1, two, k2, n1, n2, n3, n4, n5, n6, n7, out,
+):
+    nc = tc.nc
+    with ExitStack() as ctx:
+        keep = ctx.enter_context(tc.tile_pool(name="keep", bufs=1))
+        ring = ctx.enter_context(tc.tile_pool(name="ring", bufs=2))
+        psum = ctx.enter_context(tc.psum_pool(name="psum", bufs=1))
+
+        def load_list(name, src):
+            tile = keep.tile([P, S // 16], U16, name=name)
+            nc.sync.dma_start(tile[:], src)
+            return tile
+
+        def rows(src, t):
+            return src.rearrange("(p t) j -> p t j", t=PACK)[:, t, :]
+
+        ds_win = keep.tile([P, G], U8, name="ds_win")
+        xs_win = keep.tile([P, T], U8, name="xs_win")
+        ds_placed = keep.tile([P, 2 * S], U8, name="ds_placed", align_bytes=64)
+        nc.vector.memset(ds_win[:].bitcast(I32), 0)
+        nc.vector.memset(xs_win[:].bitcast(I32), 0)
+        nc.vector.memset(ds_placed[:].bitcast(I32), 0)
+
+        gm_t = keep.tile([P, PACK], F32, name="gm_t")
+        gn_t = keep.tile([P, PACK], F32, name="gn_t")
+        nc.gpsimd.dma_start(gm_t[:], gm.rearrange("(p t) o -> p (t o)", t=PACK))
+        nc.gpsimd.dma_start(gn_t[:], gn.rearrange("(p t) o -> p (t o)", t=PACK))
+
+        tab_win = [keep.tile([P, WIN], F32, name="tab_win%d" % t) for t in range(PACK)]
+        xw_win = keep.tile([P, T], I32, name="xw_win")
+        dw_win = keep.tile([P, G], I32, name="dw_win")
+
+        nc.sync.dma_start(xw_win[:], x_words[0].rearrange("p c r -> p (c r)").bitcast(I32))
+        for q in range(4):
+            nc.sync.dma_start(
+                ds_win[32 * q + SHIFT : 32 * q + SHIFT + 4, :].bitcast(I32),
+                d_scales[0, 4 * q : 4 * q + 4, :].bitcast(I32),
+            )
+        k1_l = load_list("k1_l", k1)
+        nc.sync.dma_start(tab_win[0][:, S:], rows(tab, 0))
+        n3_l = load_list("n3_l", n3)
+        k2_l = load_list("k2_l", k2)
+        n4_l = load_list("n4_l", n4)
+        offs_l = load_list("offs_l", offs)
+        nc.sync.dma_start(tab_win[1][:, S:], rows(tab, 1))
+        for q in range(4):
+            nc.sync.dma_start(
+                xs_win[32 * q : 32 * q + 4, :].bitcast(I32),
+                x_scales[0, 4 * q : 4 * q + 4, :].bitcast(I32),
+            )
+        nc.sync.dma_start(tab_win[2][:, S:], rows(tab, 2))
+        nc.sync.dma_start(dw_win[:], d_words[0].rearrange("p c r -> p (c r)").bitcast(I32))
+        nc.sync.dma_start(tab_win[3][:, S:], rows(tab, 3))
+        two_l = load_list("two_l", two)
+        n1_l = load_list("n1_l", n1)
+        n5_l = load_list("n5_l", n5)
+        n2_l = load_list("n2_l", n2)
+        n6_l = load_list("n6_l", n6)
+        n7_l = load_list("n7_l", n7)
+
+        def gather_d_scales(lst, half):
+            got = keep.tile([P, S], U8, name="ds_got%d" % half)
+            nc.vector.tensor_copy(got[:], ds_win[:].indirect(lst[:]))
+            dealt = keep.tile([P, S], U8, name="ds_dealt%d" % half, tag="late%d" % half)
+            nc.vector.tensor_copy(
+                dealt[:].rearrange("p (t m) -> p m t", t=PACK),
+                got[:].rearrange("p (m t) -> p m t", t=PACK),
+            )
+            nc.gpsimd.dma_start(
+                ds_placed[0:112, half * S : (half + 1) * S].bitcast(I32),
+                dealt[SHIFT : SHIFT + 112, :].bitcast(I32),
+            )
+
+        def load_weight(w, half):
+            raw = keep.tile([P, PACK, S], F32, name="w_raw%d" % half, tag="late%d" % half)
+            nc.sync.dma_start(raw[:], w.rearrange("(p j) c -> p j c", j=PACK))
+            return raw
+
+        def gather_x_scales(lst, half):
+            sc = keep.tile([P, S], U8, name="xs_got%d" % half, align_bytes=64)
+            nc.vector.tensor_copy(sc[:], xs_win[:].indirect(lst[:]))
+            return sc
+
+        def gather_x_words(lst, half):
+            words = keep.tile([P, S], U32, name="xw_got%d" % half, align_bytes=64)
+            nc.vector.tensor_copy(words[:], xw_win[:].bitcast(U32).indirect(lst[:]))
+            return words
+
+        def gather_d_words(lst, half):
+            got = keep.tile([P, S], U32, name="dw_got%d" % half)
+            nc.vector.tensor_copy(got[:], dw_win[:].bitcast(U32).indirect(lst[:]))
+            dealt = keep.tile([P, S], I32, name="dw_dealt%d" % half, align_bytes=64)
+            nc.vector.tensor_copy(
+                dealt[:].rearrange("p (t m) -> p m t", t=PACK),
+                got[:].bitcast(I32).rearrange("p (m t) -> p m t", t=PACK),
+            )
+            return dealt
+
+        def first_product(dealt, half, xw, xs):
+            banks = []
+            for t in range(PACK):
+                bank = psum.tile([P, S], F32, name="bank%d" % (4 * half + t))
+                nc.tensor.matmul_mx(
+                    out=bank[:],
+                    lhsT=dealt[:, t * P : (t + 1) * P].bitcast(FP8X4),
+                    lhsT_scale=ds_placed[:, half * S + t * P : half * S + (t + 1) * P],
+                    rhs=xw[:].bitcast(FP8X4),
+                    rhs_scale=xs[:],
+                    start=True,
+                    stop=True,
+                )
+                banks.append(bank)
+            return banks
+
+        def quantise(name, grouped, cols):
+            codes, scales = quantised[name]
+            nc.vector.quantize_mx(
+                out=codes[:, cols].bitcast(FP8X4),
+                scales=scales[:, cols],
+                in_=grouped[:, PACK * cols.start : PACK * cols.stop],
+            )
+
+        def round_weight(name, raw):
+            nc.vector.tensor_copy(
+                rounded[name][:].rearrange("p (t m j) -> p m j t", t=PACK, j=PACK),
+                raw[:].rearrange("p j (m t) -> p m j t", t=PACK),
+            )
+
+        def weave(name, in0, in1, op, cols):
+            nc.vector.tensor_tensor(
+                rounded[name][:, PACK * cols.start : PACK * cols.stop].rearrange("p (c i t) -> p c t i", i=4, t=PACK),
+                in0[:, :, cols].rearrange("p t (c i) -> p c t i", i=4),
+                in1[:, :, cols].rearrange("p t (c i) -> p c t i", i=4),
+                op,
+            )
+
+        rounded = {}
+        quantised = {}
+        for name in ("w1", "w2", "z", "z2"):
+            rounded[name] = keep.tile([P, PACK * S], BF16, name=name + "_rounded", align_bytes=64)
+            quantised[name] = (
+                keep.tile([P, S], U32, name=name + "_codes", align_bytes=64),
+                keep.tile([P, S], U8, name=name + "_scales", align_bytes=64),
+            )
+        whole = slice(0, S)
+        halves = (slice(0, S // 2), slice(S // 2, S))
+
+        g3 = keep.tile([P, PACK, S], F32, name="g3")
+        g4 = keep.tile([P, PACK, S], F32, name="g4")
+        g2 = keep.tile([P, PACK, S], F32, name="g2")
+        st = keep.tile([P, PACK, S], F32, name="st")
+        prod = keep.tile([P, PACK, S], F32, name="prod")
+        gn16 = keep.tile([P, PACK], F32, name="gn16")
+        gn_safe = keep.tile([P, PACK], F32, name="gn_safe")
+        gn_inv = keep.tile([P, PACK], F32, name="gn_inv")
+        tanh_win = [keep.tile([P, WIN], F32, name="tanh_win%d" % t) for t in range(PACK)]
+        tab2_win = []
+
+        def scale_tab(t):
+            nc.vector.tensor_scalar(tab_win[t][:, :S], tab_win[t][:, S:], gm_t[:, t : t + 1], None, ALU.mult)
+
+        def fetch_n3(t):
+            nc.scalar.activation(g3[:, t, :], tab_win[t][:].indirect(n3_l[:]), ACT.Copy)
+
+        def fetch_n4(t):
+            nc.scalar.activation(g4[:, t, :], tab_win[t][:].indirect(n4_l[:]), ACT.Copy)
+
+        def step_n1(t):
+            a_win = keep.tile([P, WIN], F32, name="a_win%d" % t, tag="a_tab2_win%d" % t)
+            nc.scalar.activation(a_win[:, :S], a_banks[t][:], ACT.Copy, scale=gn16[:, t : t + 1])
+            g1 = keep.tile([P, S], F32, name="g1_%d" % t)
+            nc.scalar.activation(g1[:], a_win[:].indirect(n1_l[:]), ACT.Copy)
+            win = keep.tile([P, WIN], F32, name="tab2_win%d" % t, tag="a_tab2_win%d" % t)
+            nc.sync.dma_start(win[:, :S], rows(tab2, t))
+            tab2_win.append(win)
+            return g1
+
+        def make_st(t, g1):
+            nc.vector.scalar_tensor_tensor(st[:, t, :], a_banks[t][:], gn16[:, t : t + 1], g1[:], ALU.mult, ALU.add)
+
+        def empty_b(t):
+            b_win = keep.tile([P, WIN], F32, name="b_win%d" % t, tag="b_h_win%d" % t)
+            nc.scalar.activation(b_win[:, :S], b_banks[t][:], ACT.Copy, scale=0.0625)
+            return b_win
+
+        def step_n5(t, b_win):
+            nc.vector.tensor_tensor(prod[:, t, :], b_win[:].indirect(n5_l[:]), g3[:, t, :], ALU.mult)
+
+        def make_tanh(t):
+            nc.scalar.activation(tanh_win[t][:, :S], st[:, t, :], ACT.Tanh, scale=gn_inv[:, t : t + 1])
+
+        def fetch_n2(t, cols):
+            offsets = n2_l[:, cols.start // 16 : cols.stop // 16]
+            nc.scalar.activation(g2[:, t, cols], tanh_win[t][:].indirect(offsets), ACT.Copy)
+
+        def second_product(wname, zname, cols, start, stop):
+            for t in range(PACK):
+                nc.tensor.matmul_mx(
+                    out=h_banks[t][:, cols],
+                    lhsT=quantised[wname][0][:, t * P : (t + 1) * P].bitcast(FP8X4),
+                    lhsT_scale=quantised[wname][1][:, t * P : (t + 1) * P],
+                    rhs=quantised[zname][0][:, cols].bitcast(FP8X4),
+                    rhs_scale=quantised[zname][1][:, cols],
+                    start=start,
+                    stop=stop,
+                )
+
+        gather_d_scales(k1_l, 0)
+        scale_tab(0)
+        fetch_n3(0)
+        fetch_n4(0)
+        gather_d_scales(k2_l, 1)
+        scale_tab(1)
+        fetch_n3(1)
+        fetch_n4(1)
+        xw1 = gather_x_words(offs_l, 0)
+        xs1 = gather_x_scales(offs_l, 0)
+        scale_tab(2)
+        fetch_n3(2)
+        fetch_n4(2)
+        nc.vector.tensor_scalar(gn16[:], gn_t[:], 0.0625, None, ALU.mult)
+        nc.vector.scalar_tensor_tensor(gn_safe[:], gn_t[:], 0.0, gn_t[:], ALU.is_equal, ALU.add)
+        dw1 = gather_d_words(k1_l, 0)
+        a_banks = first_product(dw1, 0, xw1, xs1)
+        scale_tab(3)
+        fetch_n3(3)
+        fetch_n4(3)
+        nc.vector.reciprocal(gn_inv[:], gn_safe[:])
+        w2_raw = load_weight(w2, 0)
+        w1_raw = load_weight(w1, 1)
+        xw2 = gather_x_words(two_l, 1)
+        xs2 = gather_x_scales(two_l, 1)
+        dw2 = gather_d_words(k2_l, 1)
+        b_banks = first_product(dw2, 1, xw2, xs2)
+
+        make_st(0, step_n1(0))
+        round_weight("w2", w2_raw)
+        make_st(1, step_n1(1))
+        quantise("w2", rounded["w2"], whole)
+        step_n5(0, empty_b(0))
+        step_n5(1, empty_b(1))
+        make_st(2, step_n1(2))
+        round_weight("w1", w1_raw)
+        step_n5(2, empty_b(2))
+        make_st(3, step_n1(3))
+        quantise("w1", rounded["w1"], whole)
+        step_n5(3, empty_b(3))
+        for t in range(PACK):
+            make_tanh(t)
+        weave("z2", prod, g4, ALU.add, whole)
+        quantise("z2", rounded["z2"], whole)
+        h_banks = [psum.tile([P, S], F32, name="bank%d" % t) for t in range(PACK)]
+        second_product("w2", "z2", whole, True, False)
+        for h, cols in enumerate(halves):
+            for t in range(PACK):
+                fetch_n2(t, cols)
+            weave("z", g2, st, ALU.mult, cols)
+            quantise("z", rounded["z"], cols)
+            second_product("w1", "z", cols, False, h == 1)
+
+        g6 = keep.tile([P, PACK, S], F32, name="g6", tag="tanh_win%d" % (PACK - 1))
+
+        def fetch_n6(t):
+            nc.scalar.activation(g6[:, t, :], tab2_win[t][:].indirect(n6_l[:]), ACT.Copy)
+
+        fetch_n6(0)
+        fetch_n6(1)
+        for t in range(PACK):
+            h_win = keep.tile([P, WIN], F32, name="h_win%d" % t, tag="b_h_win%d" % t)
+            nc.scalar.activation(h_win[:, :S], h_banks[t][:], ACT.Copy, scale=-0.5)
+            if t + 2 < PACK:
+                fetch_n6(t + 2)
+            u = ring.tile([P, S], F32, name="u")
+            nc.vector.tensor_tensor(u[:], h_banks[t][:], g6[:, t, :], ALU.mult)
+            res = keep.tile([P, S], F32, name="res%d" % t)
+            if t < PACK - 1:
+                nc.vector.tensor_tensor(res[:], h_win[:].indirect(n7_l[:]), u[:], ALU.add)
+            else:
+                g7 = keep.tile([P, S], F32, name="g7")
+                nc.scalar.activation(g7[:], h_win[:].indirect(n7_l[:]), ACT.Copy)
+                nc.vector.tensor_tensor(res[:], g7[:], u[:], ALU.add)
+            nc.sync.dma_start(rows(out, t), res[:])

@@ -29,7 +29,6 @@ def tile_picked_pqjhoppkindakindg_none_p_kernel(
     nc = tc.nc
     with ExitStack() as ctx:
         keep = ctx.enter_context(tc.tile_pool(name="keep", bufs=1))
-        ring = ctx.enter_context(tc.tile_pool(name="ring", bufs=2))
         psum = ctx.enter_context(tc.psum_pool(name="psum", bufs=1))
 
         def load_list(name, src):
@@ -49,26 +48,26 @@ def tile_picked_pqjhoppkindakindg_none_p_kernel(
 
         gm_t = keep.tile([P, PACK], F32, name="gm_t")
         gn_t = keep.tile([P, PACK], F32, name="gn_t")
-        nc.gpsimd.dma_start(gm_t[:], gm.rearrange("(p t) o -> p (t o)", t=PACK))
-        nc.gpsimd.dma_start(gn_t[:], gn.rearrange("(p t) o -> p (t o)", t=PACK))
+        nc.sync.dma_start(gm_t[:], gm.rearrange("(p t) o -> p (t o)", t=PACK))
+        nc.sync.dma_start(gn_t[:], gn.rearrange("(p t) o -> p (t o)", t=PACK))
 
         tab_win = [keep.tile([P, WIN], F32, name="tab_win%d" % t) for t in range(PACK)]
         xw_win = keep.tile([P, T], I32, name="xw_win")
         dw_win = keep.tile([P, G], I32, name="dw_win")
 
-        nc.sync.dma_start(xw_win[:], x_words[0].rearrange("p c r -> p (c r)").bitcast(I32))
+        k1_l = load_list("k1_l", k1)
         for q in range(4):
             nc.sync.dma_start(
                 ds_win[32 * q + SHIFT : 32 * q + SHIFT + 4, :].bitcast(I32),
                 d_scales[0, 4 * q : 4 * q + 4, :].bitcast(I32),
             )
-        k1_l = load_list("k1_l", k1)
         nc.sync.dma_start(tab_win[0][:, S:], rows(tab, 0))
         n3_l = load_list("n3_l", n3)
         k2_l = load_list("k2_l", k2)
         n4_l = load_list("n4_l", n4)
-        offs_l = load_list("offs_l", offs)
         nc.sync.dma_start(tab_win[1][:, S:], rows(tab, 1))
+        offs_l = load_list("offs_l", offs)
+        nc.sync.dma_start(xw_win[:], x_words[0].rearrange("p c r -> p (c r)").bitcast(I32))
         for q in range(4):
             nc.sync.dma_start(
                 xs_win[32 * q : 32 * q + 4, :].bitcast(I32),
@@ -87,6 +86,9 @@ def tile_picked_pqjhoppkindakindg_none_p_kernel(
         def gather_d_scales(lst, half):
             got = keep.tile([P, S], U8, name="ds_got%d" % half)
             nc.vector.tensor_copy(got[:], ds_win[:].indirect(lst[:]))
+            return got
+
+        def place_d_scales(got, half):
             dealt = keep.tile([P, S], U8, name="ds_dealt%d" % half, tag="late%d" % half)
             nc.vector.tensor_copy(
                 dealt[:].rearrange("p (t m) -> p m t", t=PACK),
@@ -115,6 +117,9 @@ def tile_picked_pqjhoppkindakindg_none_p_kernel(
         def gather_d_words(lst, half):
             got = keep.tile([P, S], U32, name="dw_got%d" % half)
             nc.vector.tensor_copy(got[:], dw_win[:].bitcast(U32).indirect(lst[:]))
+            return got
+
+        def deal_d_words(got, half):
             dealt = keep.tile([P, S], I32, name="dw_dealt%d" % half, align_bytes=64)
             nc.vector.tensor_copy(
                 dealt[:].rearrange("p (t m) -> p m t", t=PACK),
@@ -147,10 +152,10 @@ def tile_picked_pqjhoppkindakindg_none_p_kernel(
             )
 
         def round_weight(name, raw):
-            nc.vector.tensor_copy(
-                rounded[name][:].rearrange("p (t m j) -> p m j t", t=PACK, j=PACK),
-                raw[:].rearrange("p j (m t) -> p m j t", t=PACK),
-            )
+            dst = rounded[name][:].rearrange("p (t m j) -> p t m j", t=PACK, j=PACK)
+            src = raw[:].rearrange("p j (m t) -> p t m j", t=PACK)
+            for t in range(PACK):
+                nc.gpsimd.tensor_scalar(dst[:, t], src[:, t], 1.0, 0.0, ALU.mult, ALU.add)
 
         def weave(name, in0, in1, op, cols):
             nc.vector.tensor_tensor(
@@ -183,7 +188,7 @@ def tile_picked_pqjhoppkindakindg_none_p_kernel(
         tab2_win = []
 
         def scale_tab(t):
-            nc.vector.tensor_scalar(tab_win[t][:, :S], tab_win[t][:, S:], gm_t[:, t : t + 1], None, ALU.mult)
+            nc.gpsimd.tensor_scalar(tab_win[t][:, :S], tab_win[t][:, S:], gm_t[:, t : t + 1], 0.0, ALU.mult, ALU.add)
 
         def fetch_n3(t):
             nc.scalar.activation(g3[:, t, :], tab_win[t][:].indirect(n3_l[:]), ACT.Copy)
@@ -206,7 +211,7 @@ def tile_picked_pqjhoppkindakindg_none_p_kernel(
 
         def empty_b(t):
             b_win = keep.tile([P, WIN], F32, name="b_win%d" % t, tag="b_h_win%d" % t)
-            nc.scalar.activation(b_win[:, :S], b_banks[t][:], ACT.Copy, scale=0.0625)
+            nc.vector.tensor_scalar(b_win[:, :S], b_banks[t][:], 0.0625, None, ALU.mult)
             return b_win
 
         def step_n5(t, b_win):
@@ -231,49 +236,48 @@ def tile_picked_pqjhoppkindakindg_none_p_kernel(
                     stop=stop,
                 )
 
-        gather_d_scales(k1_l, 0)
+        nc.scalar.activation(gn16[:], gn_t[:], ACT.Copy, scale=0.0625)
         scale_tab(0)
         fetch_n3(0)
         fetch_n4(0)
-        gather_d_scales(k2_l, 1)
+        ds1 = gather_d_scales(k1_l, 0)
+        ds2 = gather_d_scales(k2_l, 1)
         scale_tab(1)
+        place_d_scales(ds1, 0)
         fetch_n3(1)
         fetch_n4(1)
         xw1 = gather_x_words(offs_l, 0)
+        place_d_scales(ds2, 1)
         xs1 = gather_x_scales(offs_l, 0)
-        scale_tab(2)
-        fetch_n3(2)
-        fetch_n4(2)
-        nc.vector.tensor_scalar(gn16[:], gn_t[:], 0.0625, None, ALU.mult)
+        for t in range(2, PACK):
+            scale_tab(t)
+            fetch_n3(t)
+            fetch_n4(t)
         nc.vector.scalar_tensor_tensor(gn_safe[:], gn_t[:], 0.0, gn_t[:], ALU.is_equal, ALU.add)
         dw1 = gather_d_words(k1_l, 0)
-        a_banks = first_product(dw1, 0, xw1, xs1)
-        scale_tab(3)
-        fetch_n3(3)
-        fetch_n4(3)
+        xw2 = gather_x_words(two_l, 1)
+        a_banks = first_product(deal_d_words(dw1, 0), 0, xw1, xs1)
         nc.vector.reciprocal(gn_inv[:], gn_safe[:])
         w2_raw = load_weight(w2, 0)
         w1_raw = load_weight(w1, 1)
-        xw2 = gather_x_words(two_l, 1)
-        xs2 = gather_x_scales(two_l, 1)
         dw2 = gather_d_words(k2_l, 1)
-        b_banks = first_product(dw2, 1, xw2, xs2)
+        xs2 = gather_x_scales(two_l, 1)
+        b_banks = first_product(deal_d_words(dw2, 1), 1, xw2, xs2)
 
-        make_st(0, step_n1(0))
         round_weight("w2", w2_raw)
-        make_st(1, step_n1(1))
-        quantise("w2", rounded["w2"], whole)
-        step_n5(0, empty_b(0))
-        step_n5(1, empty_b(1))
-        make_st(2, step_n1(2))
         round_weight("w1", w1_raw)
-        step_n5(2, empty_b(2))
-        make_st(3, step_n1(3))
-        quantise("w1", rounded["w1"], whole)
-        step_n5(3, empty_b(3))
+        b_wins = [empty_b(0)]
+        for t in range(PACK):
+            g1 = step_n1(t)
+            if t + 1 < PACK:
+                b_wins.append(empty_b(t + 1))
+            step_n5(t, b_wins[t])
+            make_st(t, g1)
         for t in range(PACK):
             make_tanh(t)
         weave("z2", prod, g4, ALU.add, whole)
+        quantise("w2", rounded["w2"], whole)
+        quantise("w1", rounded["w1"], whole)
         quantise("z2", rounded["z2"], whole)
         h_banks = [psum.tile([P, S], F32, name="bank%d" % t) for t in range(PACK)]
         second_product("w2", "z2", whole, True, False)
@@ -284,25 +288,49 @@ def tile_picked_pqjhoppkindakindg_none_p_kernel(
             quantise("z", rounded["z"], cols)
             second_product("w1", "z", cols, False, h == 1)
 
-        g6 = keep.tile([P, PACK, S], F32, name="g6", tag="tanh_win%d" % (PACK - 1))
+        g6_early = keep.tile([P, 2, S], F32, name="g6_early", tag="tanh_win%d" % (PACK - 1))
+        g6 = [g6_early[:, 0, :], g6_early[:, 1, :]]
+        for name in ("z_codes", "w1_codes"):
+            late = keep.tile([P, S], F32, name="g6_on_" + name, tag=name, align_bytes=64)
+            g6.append(late[:])
 
         def fetch_n6(t):
-            nc.scalar.activation(g6[:, t, :], tab2_win[t][:].indirect(n6_l[:]), ACT.Copy)
+            nc.scalar.activation(g6[t], tab2_win[t][:].indirect(n6_l[:]), ACT.Copy)
+
+        def empty_h(t):
+            h_win = keep.tile([P, WIN], F32, name="h_win%d" % t, tag="b_h_win%d" % t)
+            nc.scalar.activation(h_win[:, :S], h_banks[t][:], ACT.Copy, scale=-0.5)
+            return h_win
+
+        def weigh_h(t):
+            u = keep.tile([P, S], F32, name="u%d" % t)
+            nc.vector.tensor_tensor(u[:], h_banks[t][:], g6[t], ALU.mult)
+            return u
+
+        def finish(t, h_win, u, cols):
+            res = keep.tile([P, cols.stop - cols.start], F32, name="res%d_%d" % (t, cols.start))
+            offsets = n7_l[:, cols.start // 16 : cols.stop // 16]
+            nc.vector.tensor_tensor(res[:], h_win[:].indirect(offsets), u[:, cols], ALU.add)
+            nc.sync.dma_start(rows(out, t)[:, cols], res[:])
 
         fetch_n6(0)
         fetch_n6(1)
-        for t in range(PACK):
-            h_win = keep.tile([P, WIN], F32, name="h_win%d" % t, tag="b_h_win%d" % t)
-            nc.scalar.activation(h_win[:, :S], h_banks[t][:], ACT.Copy, scale=-0.5)
-            if t + 2 < PACK:
-                fetch_n6(t + 2)
-            u = ring.tile([P, S], F32, name="u")
-            nc.vector.tensor_tensor(u[:], h_banks[t][:], g6[:, t, :], ALU.mult)
-            res = keep.tile([P, S], F32, name="res%d" % t)
-            if t < PACK - 1:
-                nc.vector.tensor_tensor(res[:], h_win[:].indirect(n7_l[:]), u[:], ALU.add)
-            else:
-                g7 = keep.tile([P, S], F32, name="g7")
-                nc.scalar.activation(g7[:], h_win[:].indirect(n7_l[:]), ACT.Copy)
-                nc.vector.tensor_tensor(res[:], g7[:], u[:], ALU.add)
-            nc.sync.dma_start(rows(out, t), res[:])
+        u0 = weigh_h(0)
+        h1 = empty_h(1)
+        h0 = empty_h(0)
+        u1 = weigh_h(1)
+        fetch_n6(2)
+        h2 = empty_h(2)
+        finish(0, h0, u0, whole)
+        fetch_n6(3)
+        h3 = empty_h(3)
+        u2 = weigh_h(2)
+        finish(1, h1, u1, whole)
+        g7 = keep.tile([P, S], F32, name="g7")
+        nc.scalar.activation(g7[:], h3[:].indirect(n7_l[:]), ACT.Copy)
+        u3 = weigh_h(3)
+        finish(2, h2, u2, whole)
+        for cols in halves:
+            res = keep.tile([P, S // 2], F32, name="res3_%d" % cols.start)
+            nc.vector.tensor_tensor(res[:], g7[:, cols], u3[:, cols], ALU.add)
+            nc.sync.dma_start(rows(out, 3)[:, cols], res[:])

@@ -52,6 +52,7 @@ def tile_picked_pqjhoppkindakindg_none_p_kernel(
         nc.sync.dma_start(gn_t[:], gn.rearrange("(p t) o -> p (t o)", t=PACK))
 
         tab_win = [keep.tile([P, WIN], F32, name="tab_win%d" % t) for t in range(PACK)]
+        tab_raw = [keep.tile([P, S], F32, name="tab_raw%d" % t) for t in range(PACK)]
         xw_win = keep.tile([P, T], I32, name="xw_win")
         dw_win = keep.tile([P, G], I32, name="dw_win")
 
@@ -61,21 +62,21 @@ def tile_picked_pqjhoppkindakindg_none_p_kernel(
                 ds_win[32 * q + SHIFT : 32 * q + SHIFT + 4, :].bitcast(I32),
                 d_scales[0, 4 * q : 4 * q + 4, :].bitcast(I32),
             )
-        nc.sync.dma_start(tab_win[0][:, S:], rows(tab, 0))
+        nc.sync.dma_start(tab_raw[0][:], rows(tab, 0))
         n3_l = load_list("n3_l", n3)
         k2_l = load_list("k2_l", k2)
         n4_l = load_list("n4_l", n4)
-        nc.sync.dma_start(tab_win[1][:, S:], rows(tab, 1))
+        nc.sync.dma_start(tab_raw[1][:], rows(tab, 1))
         offs_l = load_list("offs_l", offs)
         nc.sync.dma_start(xw_win[:], x_words[0].rearrange("p c r -> p (c r)").bitcast(I32))
+        nc.sync.dma_start(tab_raw[2][:], rows(tab, 2))
+        nc.sync.dma_start(dw_win[:], d_words[0].rearrange("p c r -> p (c r)").bitcast(I32))
         for q in range(4):
             nc.sync.dma_start(
                 xs_win[32 * q : 32 * q + 4, :].bitcast(I32),
                 x_scales[0, 4 * q : 4 * q + 4, :].bitcast(I32),
             )
-        nc.sync.dma_start(tab_win[2][:, S:], rows(tab, 2))
-        nc.sync.dma_start(dw_win[:], d_words[0].rearrange("p c r -> p (c r)").bitcast(I32))
-        nc.sync.dma_start(tab_win[3][:, S:], rows(tab, 3))
+        nc.sync.dma_start(tab_raw[3][:], rows(tab, 3))
         two_l = load_list("two_l", two)
         n1_l = load_list("n1_l", n1)
         n5_l = load_list("n5_l", n5)
@@ -83,24 +84,21 @@ def tile_picked_pqjhoppkindakindg_none_p_kernel(
         n6_l = load_list("n6_l", n6)
         n7_l = load_list("n7_l", n7)
 
-        def gather_d_scales(lst, half):
-            got = keep.tile([P, S], U8, name="ds_got%d" % half)
+        ds_dealt = keep.tile([P, 2 * S], U8, name="ds_dealt", tag="then_w2")
+
+        def gather_d_scales(lst, half, tag):
+            got = keep.tile([P, S], U8, name="ds_got%d" % half, tag=tag)
             nc.vector.tensor_copy(got[:], ds_win[:].indirect(lst[:]))
             return got
 
-        def place_d_scales(got, half):
-            dealt = keep.tile([P, S], U8, name="ds_dealt%d" % half, tag="late%d" % half)
+        def deal_d_scales(got, half):
             nc.vector.tensor_copy(
-                dealt[:].rearrange("p (t m) -> p m t", t=PACK),
+                ds_dealt[:, half * S : (half + 1) * S].rearrange("p (t m) -> p m t", t=PACK),
                 got[:].rearrange("p (m t) -> p m t", t=PACK),
             )
-            nc.gpsimd.dma_start(
-                ds_placed[0:112, half * S : (half + 1) * S].bitcast(I32),
-                dealt[SHIFT : SHIFT + 112, :].bitcast(I32),
-            )
 
-        def load_weight(w, half):
-            raw = keep.tile([P, PACK, S], F32, name="w_raw%d" % half, tag="late%d" % half)
+        def load_weight(w, tag):
+            raw = keep.tile([P, PACK, S], F32, name="raw_" + tag, tag=tag)
             nc.sync.dma_start(raw[:], w.rearrange("(p j) c -> p j c", j=PACK))
             return raw
 
@@ -114,8 +112,8 @@ def tile_picked_pqjhoppkindakindg_none_p_kernel(
             nc.vector.tensor_copy(words[:], xw_win[:].bitcast(U32).indirect(lst[:]))
             return words
 
-        def gather_d_words(lst, half):
-            got = keep.tile([P, S], U32, name="dw_got%d" % half)
+        def gather_d_words(lst, half, tag):
+            got = keep.tile([P, S], U32, name="dw_got%d" % half, tag=tag)
             nc.vector.tensor_copy(got[:], dw_win[:].bitcast(U32).indirect(lst[:]))
             return got
 
@@ -152,10 +150,10 @@ def tile_picked_pqjhoppkindakindg_none_p_kernel(
             )
 
         def round_weight(name, raw):
-            dst = rounded[name][:].rearrange("p (t m j) -> p t m j", t=PACK, j=PACK)
-            src = raw[:].rearrange("p j (m t) -> p t m j", t=PACK)
-            for t in range(PACK):
-                nc.gpsimd.tensor_scalar(dst[:, t], src[:, t], 1.0, 0.0, ALU.mult, ALU.add)
+            nc.vector.tensor_copy(
+                rounded[name][:].rearrange("p (t m j) -> p m j t", t=PACK, j=PACK),
+                raw[:].rearrange("p j (m t) -> p m j t", t=PACK),
+            )
 
         def weave(name, in0, in1, op, cols):
             nc.vector.tensor_tensor(
@@ -188,7 +186,10 @@ def tile_picked_pqjhoppkindakindg_none_p_kernel(
         tab2_win = []
 
         def scale_tab(t):
-            nc.gpsimd.tensor_scalar(tab_win[t][:, :S], tab_win[t][:, S:], gm_t[:, t : t + 1], 0.0, ALU.mult, ALU.add)
+            if t == 0:
+                nc.scalar.activation(tab_win[t][:, :S], tab_raw[t][:], ACT.Copy, scale=gm_t[:, t : t + 1])
+            else:
+                nc.vector.tensor_scalar(tab_win[t][:, :S], tab_raw[t][:], gm_t[:, t : t + 1], None, ALU.mult)
 
         def fetch_n3(t):
             nc.scalar.activation(g3[:, t, :], tab_win[t][:].indirect(n3_l[:]), ACT.Copy)
@@ -211,7 +212,10 @@ def tile_picked_pqjhoppkindakindg_none_p_kernel(
 
         def empty_b(t):
             b_win = keep.tile([P, WIN], F32, name="b_win%d" % t, tag="b_h_win%d" % t)
-            nc.vector.tensor_scalar(b_win[:, :S], b_banks[t][:], 0.0625, None, ALU.mult)
+            if t == 0:
+                nc.vector.tensor_scalar(b_win[:, :S], b_banks[t][:], 0.0625, None, ALU.mult)
+            else:
+                nc.scalar.activation(b_win[:, :S], b_banks[t][:], ACT.Copy, scale=0.0625)
             return b_win
 
         def step_n5(t, b_win):
@@ -240,33 +244,36 @@ def tile_picked_pqjhoppkindakindg_none_p_kernel(
         scale_tab(0)
         fetch_n3(0)
         fetch_n4(0)
-        ds1 = gather_d_scales(k1_l, 0)
-        ds2 = gather_d_scales(k2_l, 1)
+        ds1 = gather_d_scales(k1_l, 0, "ds_got0")
+        ds2 = gather_d_scales(k2_l, 1, "then_w1")
         scale_tab(1)
-        place_d_scales(ds1, 0)
+        deal_d_scales(ds1, 0)
         fetch_n3(1)
         fetch_n4(1)
         xw1 = gather_x_words(offs_l, 0)
-        place_d_scales(ds2, 1)
+        deal_d_scales(ds2, 1)
+        nc.sync.dma_start(ds_placed[0:112, :].bitcast(I32), ds_dealt[SHIFT : SHIFT + 112, :].bitcast(I32))
+        scale_tab(2)
+        fetch_n3(2)
+        fetch_n4(2)
+        dw1 = gather_d_words(k1_l, 0, "dw_got0")
         xs1 = gather_x_scales(offs_l, 0)
-        for t in range(2, PACK):
-            scale_tab(t)
-            fetch_n3(t)
-            fetch_n4(t)
-        nc.vector.scalar_tensor_tensor(gn_safe[:], gn_t[:], 0.0, gn_t[:], ALU.is_equal, ALU.add)
-        dw1 = gather_d_words(k1_l, 0)
-        xw2 = gather_x_words(two_l, 1)
         a_banks = first_product(deal_d_words(dw1, 0), 0, xw1, xs1)
+        scale_tab(3)
+        fetch_n3(3)
+        fetch_n4(3)
+        nc.vector.scalar_tensor_tensor(gn_safe[:], gn_t[:], 0.0, gn_t[:], ALU.is_equal, ALU.add)
+        xw2 = gather_x_words(two_l, 1)
         nc.vector.reciprocal(gn_inv[:], gn_safe[:])
-        w2_raw = load_weight(w2, 0)
-        w1_raw = load_weight(w1, 1)
-        dw2 = gather_d_words(k2_l, 1)
+        w2_raw = load_weight(w2, "then_w2")
+        w1_raw = load_weight(w1, "then_w1")
+        dw2 = gather_d_words(k2_l, 1, "tab_raw%d" % (PACK - 1))
         xs2 = gather_x_scales(two_l, 1)
         b_banks = first_product(deal_d_words(dw2, 1), 1, xw2, xs2)
 
-        round_weight("w2", w2_raw)
         round_weight("w1", w1_raw)
         b_wins = [empty_b(0)]
+        round_weight("w2", w2_raw)
         for t in range(PACK):
             g1 = step_n1(t)
             if t + 1 < PACK:

from contextlib import ExitStack

import concourse.mybir as mybir

F32 = mybir.dt.float32
BF16 = mybir.dt.bfloat16
I32 = mybir.dt.int32
U32 = mybir.dt.uint32
U16 = mybir.dt.uint16
U8 = mybir.dt.uint8
FP8X4 = mybir.dt.float8_e4m3fn_x4
ALU = mybir.AluOpType
ACT = mybir.ActivationFunctionType

P = 128
PACK = 4
S = 512
T = 1024
G = 2048
WIN = 1024
SHIFT = 14
FLOPS = 4 * 2 * 512 * 512 * 512


def tile_picked_pqjhoppkindakindg_none_p_kernel(
    tc, x_words, x_scales, d_words, d_scales, tab, gn, gm, w1, w2, tab2,
    offs, k1, two, k2, n1, n2, n3, n4, n5, n6, n7, out,
):
    nc = tc.nc
    with ExitStack() as ctx:
        keep = ctx.enter_context(tc.tile_pool(name="keep", bufs=1))
        psum = ctx.enter_context(tc.psum_pool(name="psum", bufs=1))

        def load_list(name, src):
            tile = keep.tile([P, S // 16], U16, name=name)
            nc.sync.dma_start(tile[:], src)
            return tile

        def rows(src, t):
            return src.rearrange("(p t) j -> p t j", t=PACK)[:, t, :]

        ds_win = keep.tile([P, G], U8, name="ds_win")
        xs_win = keep.tile([P, T], U8, name="xs_win")
        ds_placed = keep.tile([P, 2 * S], U8, name="ds_placed", align_bytes=64)
        nc.vector.memset(ds_win[:].bitcast(I32), 0)
        nc.vector.memset(xs_win[:].bitcast(I32), 0)
        nc.vector.memset(ds_placed[:].bitcast(I32), 0)

        gm_t = keep.tile([P, PACK], F32, name="gm_t")
        gn_t = keep.tile([P, PACK], F32, name="gn_t")
        nc.sync.dma_start(gm_t[:], gm.rearrange("(p t) o -> p (t o)", t=PACK))
        nc.sync.dma_start(gn_t[:], gn.rearrange("(p t) o -> p (t o)", t=PACK))

        tab_win = [keep.tile([P, WIN], F32, name="tab_win%d" % t) for t in range(PACK)]
        tab_raw = [keep.tile([P, S], F32, name="tab_raw%d" % t) for t in range(PACK)]
        xw_win = keep.tile([P, T], I32, name="xw_win")
        dw_win = keep.tile([P, G], I32, name="dw_win")

        k1_l = load_list("k1_l", k1)
        for q in range(4):
            nc.sync.dma_start(
                ds_win[32 * q + SHIFT : 32 * q + SHIFT + 4, :].bitcast(I32),
                d_scales[0, 4 * q : 4 * q + 4, :].bitcast(I32),
            )
        nc.sync.dma_start(tab_raw[0][:], rows(tab, 0))
        n3_l = load_list("n3_l", n3)
        k2_l = load_list("k2_l", k2)
        n4_l = load_list("n4_l", n4)
        nc.sync.dma_start(tab_raw[1][:], rows(tab, 1))
        offs_l = load_list("offs_l", offs)
        nc.sync.dma_start(xw_win[:], x_words[0].rearrange("p c r -> p (c r)").bitcast(I32))
        nc.sync.dma_start(tab_raw[2][:], rows(tab, 2))
        nc.sync.dma_start(dw_win[:], d_words[0].rearrange("p c r -> p (c r)").bitcast(I32))
        for q in range(4):
            nc.sync.dma_start(
                xs_win[32 * q : 32 * q + 4, :].bitcast(I32),
                x_scales[0, 4 * q : 4 * q + 4, :].bitcast(I32),
            )
        nc.sync.dma_start(tab_raw[3][:], rows(tab, 3))
        two_l = load_list("two_l", two)
        n1_l = load_list("n1_l", n1)
        n5_l = load_list("n5_l", n5)
        n2_l = load_list("n2_l", n2)
        n6_l = load_list("n6_l", n6)
        n7_l = load_list("n7_l", n7)

        ds_dealt = keep.tile([P, 2 * S], U8, name="ds_dealt", tag="then_w2")

        def gather_d_scales(lst, half, tag):
            got = keep.tile([P, S], U8, name="ds_got%d" % half, tag=tag)
            nc.vector.tensor_copy(got[:], ds_win[:].indirect(lst[:]))
            return got

        def deal_d_scales(got, half):
            nc.vector.tensor_copy(
                ds_dealt[:, half * S : (half + 1) * S].rearrange("p (t m) -> p m t", t=PACK),
                got[:].rearrange("p (m t) -> p m t", t=PACK),
            )

        def load_weight(w, tag):
            raw = keep.tile([P, PACK, S], F32, name="raw_" + tag, tag=tag)
            nc.sync.dma_start(raw[:], w.rearrange("(p j) c -> p j c", j=PACK))
            return raw

        def gather_x_scales(lst, half):
            sc = keep.tile([P, S], U8, name="xs_got%d" % half, align_bytes=64)
            nc.vector.tensor_copy(sc[:], xs_win[:].indirect(lst[:]))
            return sc

        def gather_x_words(lst, half):
            words = keep.tile([P, S], U32, name="xw_got%d" % half, align_bytes=64)
            nc.vector.tensor_copy(words[:], xw_win[:].bitcast(U32).indirect(lst[:]))
            return words

        def gather_d_words(lst, half, tag):
            got = keep.tile([P, S], U32, name="dw_got%d" % half, tag=tag)
            nc.vector.tensor_copy(got[:], dw_win[:].bitcast(U32).indirect(lst[:]))
            return got

        def deal_d_words(got, half):
            dealt = keep.tile([P, S], I32, name="dw_dealt%d" % half, align_bytes=64)
            nc.vector.tensor_copy(
                dealt[:].rearrange("p (t m) -> p m t", t=PACK),
                got[:].bitcast(I32).rearrange("p (m t) -> p m t", t=PACK),
            )
            return dealt

        def first_product(dealt, half, xw, xs):
            banks = []
            for t in range(PACK):
                bank = psum.tile([P, S], F32, name="bank%d" % (4 * half + t))
                nc.tensor.matmul_mx(
                    out=bank[:],
                    lhsT=dealt[:, t * P : (t + 1) * P].bitcast(FP8X4),
                    lhsT_scale=ds_placed[:, half * S + t * P : half * S + (t + 1) * P],
                    rhs=xw[:].bitcast(FP8X4),
                    rhs_scale=xs[:],
                    start=True,
                    stop=True,
                )
                banks.append(bank)
            return banks

        def quantise(name, grouped, cols):
            codes, scales = quantised[name]
            nc.vector.quantize_mx(
                out=codes[:, cols].bitcast(FP8X4),
                scales=scales[:, cols],
                in_=grouped[:, PACK * cols.start : PACK * cols.stop],
            )

        def round_weight(name, raw):
            nc.vector.tensor_copy(
                rounded[name][:].rearrange("p (t m j) -> p m j t", t=PACK, j=PACK),
                raw[:].rearrange("p j (m t) -> p m j t", t=PACK),
            )

        def weave(name, in0, in1, op, cols):
            nc.vector.tensor_tensor(
                rounded[name][:, PACK * cols.start : PACK * cols.stop].rearrange("p (c i t) -> p c t i", i=4, t=PACK),
                in0[:, :, cols].rearrange("p t (c i) -> p c t i", i=4),
                in1[:, :, cols].rearrange("p t (c i) -> p c t i", i=4),
                op,
            )

        rounded = {}
        quantised = {}
        for name in ("w1", "w2", "z", "z2"):
            rounded[name] = keep.tile([P, PACK * S], BF16, name=name + "_rounded", align_bytes=64)
            quantised[name] = (
                keep.tile([P, S], U32, name=name + "_codes", align_bytes=64),
                keep.tile([P, S], U8, name=name + "_scales", align_bytes=64),
            )
        whole = slice(0, S)
        halves = (slice(0, S // 2), slice(S // 2, S))

        g3 = keep.tile([P, PACK, S], F32, name="g3")
        g4 = keep.tile([P, PACK, S], F32, name="g4")
        g2 = keep.tile([P, PACK, S], F32, name="g2")
        st = keep.tile([P, PACK, S], F32, name="st")
        prod = keep.tile([P, PACK, S], F32, name="prod")
        gn16 = keep.tile([P, PACK], F32, name="gn16")
        gn_safe = keep.tile([P, PACK], F32, name="gn_safe")
        gn_inv = keep.tile([P, PACK], F32, name="gn_inv")
        tanh_win = [keep.tile([P, WIN], F32, name="tanh_win%d" % t) for t in range(PACK)]
        tab2_win = []

        def scale_tab(t):
            if t == 0:
                nc.scalar.activation(tab_win[t][:, :S], tab_raw[t][:], ACT.Copy, scale=gm_t[:, t : t + 1])
            else:
                nc.vector.tensor_scalar(tab_win[t][:, :S], tab_raw[t][:], gm_t[:, t : t + 1], None, ALU.mult)

        def fetch_n3(t):
            nc.scalar.activation(g3[:, t, :], tab_win[t][:].indirect(n3_l[:]), ACT.Copy)

        def fetch_n4(t):
            nc.scalar.activation(g4[:, t, :], tab_win[t][:].indirect(n4_l[:]), ACT.Copy)

        def step_n1(t):
            a_win = keep.tile([P, WIN], F32, name="a_win%d" % t, tag="a_tab2_win%d" % t)
            nc.scalar.activation(a_win[:, :S], a_banks[t][:], ACT.Copy, scale=gn16[:, t : t + 1])
            g1 = keep.tile([P, S], F32, name="g1_%d" % t)
            nc.scalar.activation(g1[:], a_win[:].indirect(n1_l[:]), ACT.Copy)
            win = keep.tile([P, WIN], F32, name="tab2_win%d" % t, tag="a_tab2_win%d" % t)
            nc.sync.dma_start(win[:, :S], rows(tab2, t))
            tab2_win.append(win)
            return g1

        def make_st(t, g1):
            nc.vector.scalar_tensor_tensor(st[:, t, :], a_banks[t][:], gn16[:, t : t + 1], g1[:], ALU.mult, ALU.add)

        def empty_b(t):
            b_win = keep.tile([P, WIN], F32, name="b_win%d" % t, tag="b_h_win%d" % t)
            if t == 0:
                nc.vector.tensor_scalar(b_win[:, :S], b_banks[t][:], 0.0625, None, ALU.mult)
            else:
                nc.scalar.activation(b_win[:, :S], b_banks[t][:], ACT.Copy, scale=0.0625)
            return b_win

        def step_n5(t, b_win):
            nc.vector.tensor_tensor(prod[:, t, :], b_win[:].indirect(n5_l[:]), g3[:, t, :], ALU.mult)

        def make_tanh(t):
            nc.scalar.activation(tanh_win[t][:, :S], st[:, t, :], ACT.Tanh, scale=gn_inv[:, t : t + 1])

        def fetch_n2(t, cols):
            offsets = n2_l[:, cols.start // 16 : cols.stop // 16]
            nc.scalar.activation(g2[:, t, cols], tanh_win[t][:].indirect(offsets), ACT.Copy)

        def second_product(wname, zname, cols, start, stop):
            for t in range(PACK):
                nc.tensor.matmul_mx(
                    out=h_banks[t][:, cols],
                    lhsT=quantised[wname][0][:, t * P : (t + 1) * P].bitcast(FP8X4),
                    lhsT_scale=quantised[wname][1][:, t * P : (t + 1) * P],
                    rhs=quantised[zname][0][:, cols].bitcast(FP8X4),
                    rhs_scale=quantised[zname][1][:, cols],
                    start=start,
                    stop=stop,
                )

        nc.scalar.activation(gn16[:], gn_t[:], ACT.Copy, scale=0.0625)
        scale_tab(0)
        fetch_n3(0)
        fetch_n4(0)
        ds1 = gather_d_scales(k1_l, 0, "ds_got0")
        ds2 = gather_d_scales(k2_l, 1, "then_w1")
        scale_tab(1)
        deal_d_scales(ds1, 0)
        fetch_n3(1)
        fetch_n4(1)
        xw1 = gather_x_words(offs_l, 0)
        deal_d_scales(ds2, 1)
        nc.sync.dma_start(ds_placed[0:112, :].bitcast(I32), ds_dealt[SHIFT : SHIFT + 112, :].bitcast(I32))
        scale_tab(2)
        fetch_n3(2)
        fetch_n4(2)
        dw1 = gather_d_words(k1_l, 0, "dw_got0")
        xs1 = gather_x_scales(offs_l, 0)
        a_banks = first_product(deal_d_words(dw1, 0), 0, xw1, xs1)
        scale_tab(3)
        fetch_n3(3)
        fetch_n4(3)
        nc.vector.scalar_tensor_tensor(gn_safe[:], gn_t[:], 0.0, gn_t[:], ALU.is_equal, ALU.add)
        xw2 = gather_x_words(two_l, 1)
        nc.vector.reciprocal(gn_inv[:], gn_safe[:])
        w2_raw = load_weight(w2, "then_w2")
        w1_raw = load_weight(w1, "then_w1")
        dw2 = gather_d_words(k2_l, 1, "tab_raw%d" % (PACK - 1))
        xs2 = gather_x_scales(two_l, 1)
        b_banks = first_product(deal_d_words(dw2, 1), 1, xw2, xs2)

        round_weight("w1", w1_raw)
        b_wins = [empty_b(0)]
        round_weight("w2", w2_raw)
        for t in range(PACK):
            g1 = step_n1(t)
            if t + 1 < PACK:
                b_wins.append(empty_b(t + 1))
            step_n5(t, b_wins[t])
            make_st(t, g1)
        for t in range(PACK):
            make_tanh(t)
        weave("z2", prod, g4, ALU.add, whole)
        quantise("w2", rounded["w2"], whole)
        quantise("w1", rounded["w1"], whole)
        quantise("z2", rounded["z2"], whole)
        h_banks = [psum.tile([P, S], F32, name="bank%d" % t) for t in range(PACK)]
        second_product("w2", "z2", whole, True, False)
        for h, cols in enumerate(halves):
            for t in range(PACK):
                fetch_n2(t, cols)
            weave("z", g2, st, ALU.mult, cols)
            quantise("z", rounded["z"], cols)
            second_product("w1", "z", cols, False, h == 1)

        g6_early = keep.tile([P, 2, S], F32, name="g6_early", tag="tanh_win%d" % (PACK - 1))
        g6 = [g6_early[:, 0, :], g6_early[:, 1, :]]
        for name in ("z_codes", "w1_codes"):
            late = keep.tile([P, S], F32, name="g6_on_" + name, tag=name, align_bytes=64)
            g6.append(late[:])

        def fetch_n6(t):
            nc.scalar.activation(g6[t], tab2_win[t][:].indirect(n6_l[:]), ACT.Copy)

        def empty_h(t):
            h_win = keep.tile([P, WIN], F32, name="h_win%d" % t, tag="b_h_win%d" % t)
            nc.scalar.activation(h_win[:, :S], h_banks[t][:], ACT.Copy, scale=-0.5)
            return h_win

        def weigh_h(t):
            u = keep.tile([P, S], F32, name="u%d" % t)
            nc.vector.tensor_tensor(u[:], h_banks[t][:], g6[t], ALU.mult)
            return u

        def finish(t, h_win, u, cols):
            res = keep.tile([P, cols.stop - cols.start], F32, name="res%d_%d" % (t, cols.start))
            offsets = n7_l[:, cols.start // 16 : cols.stop // 16]
            nc.vector.tensor_tensor(res[:], h_win[:].indirect(offsets), u[:, cols], ALU.add)
            nc.sync.dma_start(rows(out, t)[:, cols], res[:])

        fetch_n6(0)
        fetch_n6(1)
        u0 = weigh_h(0)
        h1 = empty_h(1)
        h0 = empty_h(0)
        u1 = weigh_h(1)
        fetch_n6(2)
        h2 = empty_h(2)
        finish(0, h0, u0, whole)
        fetch_n6(3)
        h3 = empty_h(3)
        u2 = weigh_h(2)
        finish(1, h1, u1, whole)
        g7 = keep.tile([P, S], F32, name="g7")
        nc.scalar.activation(g7[:], h3[:].indirect(n7_l[:]), ACT.Copy)
        u3 = weigh_h(3)
        finish(2, h2, u2, whole)
        for cols in halves:
            res = keep.tile([P, S // 2], F32, name="res3_%d" % cols.start)
            nc.vector.tensor_tensor(res[:], g7[:, cols], u3[:, cols], ALU.add)
            nc.sync.dma_start(rows(out, 3)[:, cols], res[:])
